import numpy as np, ml_dtypes
CORES = [2,6,10,14,18,22,26,30]
N = 8
BF = ml_dtypes.bfloat16
def gentries(a):
    return np.ascontiguousarray(a.reshape(8, 16, -1).transpose(0, 2, 1)).reshape(8, -1)
def gtable(e):
    e = np.asarray(e); return np.ascontiguousarray(e.reshape(8, -1, 16).transpose(0, 2, 1)).reshape(128, -1).astype(np.int32)
W, C, RO, K = 4096, 256, 3, 5
M = W - 1
def parts(rng):
    ct = rng.integers(0, W, (N, 8, 16, C)); bk = (16 * rng.random((N, 8, 1, W)) * rng.random((N, 8, 16, W))).astype(np.int64)
    pr = rng.integers(0, 241, (N, 8, 16, C)); pg = rng.integers(0, C, (N, 8, C))
    a = rng.integers(0, W, (N, 8, C)); th = rng.integers(500, 1100, (N, 8, C))
    return ct, bk, pr, pg, a, th
def pack(ct, bk, pr, pg, a, th):
    return {"ct": np.ascontiguousarray(ct.reshape(N, 128, C)).astype(np.int32), "bk": np.ascontiguousarray(bk.reshape(N, 128, W)).astype(np.float32).astype(BF),
            "pr": np.ascontiguousarray(pr.reshape(N, 128, C)).astype(np.int32), "pg": np.stack([gtable(x) for x in pg]), "a0": a.astype(np.int32), "th": th.astype(np.int32)}
def setup_inputs(rng):
    return pack(*parts(rng))
def setup_inputs_ties(rng):
    ct, bk, pr, pg, a, th = parts(rng)
    bk = (rng.random((N, 8, 16, W)) < rng.choice(np.array([0.02, 0.05, 0.1]), (N, 8, 1, 1))).astype(np.int64)
    pr = rng.integers(0, 3, (N, 8, 16, C)); th = rng.integers(0, 20, (N, 8, C))
    pr[:, 1::2] = np.minimum(pr[:, 1::2] + 1, 2)
    bk[:, 0] = rng.integers(1, 5, (N, 16, W)); th[:, 0] = np.add.reduce(pr[:, 0], axis=1) + rng.integers(0, 2, (N, C))
    return pack(ct, bk, pr, pg, a, th)
def setup_inputs_ends(rng):
    ct, bk, pr, pg, a, th = parts(rng); e = np.array([0, 1, W // 2, M - 1, M])
    ct[:, ::2] = e[rng.integers(0, 5, (N, 4, 16, C))]; a[:, ::2] = e[rng.integers(0, 5, (N, 4, C))]
    ct[:, 4, :, ::2] = rng.integers(0, W, (N, 16, C // 2))
    ct[:, 1] = ct[:, 1, :1]
    pg[:, 5] = rng.integers(0, C, (N, 1)); pg[:, 6] = rng.choice(np.array([0, C - 1]), (N, C)); pg[:, 0] = rng.choice(np.array([0, C - 1, 1]), (N, C))
    th = np.where(rng.random(th.shape) < 0.5, th, rng.choice(np.array([0, 4095]), th.shape))
    a[:, 3] = a[:1, 3]; ct[:, 3] = (rng.permutation(W).reshape(16, C) + a[:, 3, None]) & M; pg[:, 3] = np.arange(C); th[:, 3] = 0
    low = int(rng.integers(0, 2)) * (C // 2); dd = low + np.arange(0, C // 2, 2)
    s7 = 16 * (low + 1 + 2 * rng.integers(0, C // 4, (16, C))) + rng.integers(0, 16, (16, C))
    s7[0, dd] = 16 * dd + 1; s7[1, dd] = 16 * dd + 16
    a[:, 7] = a[:1, 7]; ct[:, 7] = (s7 + a[:, 7, None]) & M; pg[:, 7] = np.arange(C); pr[:, 7] = 240
    b7 = bk[:, 7]; b7[:, :, 16 * dd + 1] = rng.integers(9, 16, (N, 16, len(dd))); b7[:, :, 16 * dd + 16] = 0
    v7 = worth(bk[:, 7:8], ((ct - a[:, :, None, :]) & M)[:, 7:8], pr[:, 7:8])[:, 0]
    th[:, 7] = 4095; t7 = th[:, 7]; t7[:, dd] = v7[:, dd] - 16 * rng.integers(0, 2, (N, len(dd)))
    return pack(ct, bk, pr, pg, a, th)
def setup_inputs_full(rng):
    ct, bk, pr, pg, a, th = parts(rng)
    bk[:, ::2] = 15 - rng.integers(0, 4, (N, 4, 16, W)) * (rng.random((N, 4, 16, W)) < 0.1)
    ct[:, 0] &= ~1; a[:, 0] &= ~1
    bk[:, 0, :, 0::2] = 15; bk[:, 0, :, 1::2] = rng.integers(3, 11, (N, 16, W // 2))
    pr[:, ::2] = rng.choice(np.array([240, 240, 239, 238, 232, 225]), (N, 4, 16, C)); pr[:, 0, :, ::2] = 240
    th[:, ::2] = rng.integers(3660, 3820, (N, 4, C)); th[:, 0] = rng.choice(np.array([3800, 3839, 3840, 3841]), (N, C))
    th[:, 0, 0] = 3840; th[:, 0, 2] = 3841
    pr[:, 4, :, 1::2] = 0; th[:, 4, 1::2] = rng.integers(0, 2, (N, C // 2))
    z = W // 4; s1 = rng.integers(0, z, (N, 16, C)); s1[:, 14] = 0; s1[:, 15] = z - 1
    ct[:, 1] = (s1 + a[:, 1, None]) & M; bk[:, 1, :, :z] = 0; bk[:, 1, :, z:] = rng.integers(1, 16, (N, 16, W - z))
    pg[:, 1] = np.argsort(rng.random((N, C)), axis=-1)
    return pack(ct, bk, pr, pg, a, th)
def setup_inputs_crib(rng):
    ct, bk, pr, pg, a, th = parts(rng)
    words = rng.integers(0, W, (8, 16, 4)); plain = np.take_along_axis(words[None], rng.integers(0, 4, (N, 8, 16, C)), 3)
    plain = np.where(rng.random(plain.shape) < 0.25, rng.integers(0, W, plain.shape), plain)
    hs = rng.permutation(W)[:W // 8]; plain[:, 5] = hs[rng.integers(0, W // 8, (N, 16, C))]; plain[:, 5, int(rng.integers(0, K))] = hs[0]
    true = rng.integers(0, W, (N, 8, C)); ct = (plain + true[:, :, None, :]) & M
    a = np.where(rng.random(a.shape) < 0.5, true, a)
    a[:, 5] = true[:, 5]; a[0::2, 5] = (true[0::2, 5] + rng.integers(1, W, true[0::2, 5].shape)) & M
    hot = np.zeros((8, W), bool); hot[np.arange(8)[:, None], words.reshape(8, -1)] = True
    hot[5] = False; hot[5, hs] = True
    bk = np.where(hot[None, :, None, :], rng.integers(7, 16, bk.shape), rng.integers(0, 4, bk.shape))
    th = rng.integers(300, 1700, th.shape); th[:, 7] = 4095
    return pack(ct, bk, pr, pg, a, th)
def setup_inputs_spread(rng):
    ct, bk, pr, pg, a, th = parts(rng)
    ex = rng.choice(np.array([0.2, 1.0, 4.0, 12.0]), (N, 8, 1, W)) * rng.choice(np.array([0.5, 1.0, 2.0]), (N, 8, 16, 1))
    bk = np.minimum((16 * rng.random((N, 8, 16, W)) ** ex).astype(np.int64), 15)
    pr = np.minimum(np.exp2(8 * rng.random((N, 8, 16, C))).astype(np.int64) - 1, 240)
    ct = (ct[:, :, :1] + (np.exp2(12 * rng.random((N, 8, 1, C))) * rng.random((N, 8, 16, C))).astype(np.int64)) & M
    pg = (C * rng.random((N, 8, C)) ** rng.choice(np.array([1.0, 3.0, 8.0]), (N, 8, 1))).astype(np.int64) % C
    th = np.minimum(np.exp2(12 * rng.random((N, 8, C))).astype(np.int64) - 1, 4095)
    return pack(ct, bk, pr, pg, a, th)
def check_inputs(d):
    bad = []
    for k, lo, hi in (("ct", 0, W - 1), ("pr", 0, 240), ("pg", 0, C - 1), ("a0", 0, W - 1), ("th", 0, 4095)):
        if np.min(d[k]) < lo or np.max(d[k]) > hi: bad.append("range of " + k)
    b = np.asarray(d["bk"]).astype(np.float32)
    if np.any(b != np.floor(b)): bad.append("bk holds whole numbers")
    if np.min(b) < 0 or np.max(b) > 15: bad.append("range of bk")
    return bad
def worth(b, s, cap):
    w = np.zeros(cap.shape, np.int32)
    for i in range(16): w = w + np.take_along_axis(b, s[:, :, i:i + 1], 3)
    return np.add.reduce(np.minimum(w, cap), axis=2)
def reference(ct, bk, pr, pg, a0, th):
    x = ct.astype(np.int64).reshape(N, 8, 16, C); cap = pr.astype(np.int32).reshape(N, 8, 16, C)
    b = bk.astype(np.float32).astype(np.int32).reshape(N, 8, 16, W); a = a0.astype(np.int64)
    f = np.stack([gentries(e) for e in pg]).astype(np.int64)
    for t in range(RO):
        s = (x - a[:, :, None, :]) & M
        other = s[[(r + 1 + t % (N - 1)) % N for r in range(N)]]
        z = np.take_along_axis(other, f[:, :, None, :], 3)
        v = worth(b, s, cap); best = a
        for k in range(1, K + 1):
            i = K * t + k - 1
            ak = (x[:, :, i] - z[:, :, i]) & M
            vk = worth(b, (x - ak[:, :, None, :]) & M, cap)
            best = np.where(vk > v, ak, best); v = np.maximum(v, vk)
        a = best
        s = (x - a[:, :, None, :]) & M
        got = np.take_along_axis(b, s.transpose(0, 1, 3, 2).reshape(N, 8, 1, W), 3)
        on = np.repeat(v >= th, 16, axis=2)[:, :, None, :]
        b = np.where(on, b + np.sign(got - b), b)
    return {"ya": a.astype(np.float32), "yv": v.astype(np.float32), "yb": b.reshape(N, 128, W).astype(np.float32).astype(BF)}

from concourse.mybir import AluOpType, ActivationFunctionType

N = 8
RO = 3
BIG = 1 << 23


def C(c):
    return 128 + 80 * c


ORDER = """
1own 0own 0A0 0sz 0e 0mm 0k7 0k4 0k6 0k5 0k2 0y0 0y1 0y2 1A0 0y3 0y4 0k1 0and1 0and0 0u1 0u0 1e 0V1 1mm 0s4 1y3 0V2
1y4 1y0 1y1 1y2 0r4 0V3 0k8 0V0 1and0 0A1 0s0 0A2 0rz 0r0 0A3 0A4 0s5 0s2 0s6 0r5 0s3 1u0 0r3 0k3 1V3 0r6 0r2 0s7 0r7
0bs0 1V0 1A1 0sc0 0ki0 0kl0 0ku0 0gl0 0gb0 0send 0lg0 0cl0 0lg1 0cl1 0ac0 0ac1 0sw 0lg2 1V1 0cl2 0ac2 0x0 0x1 1sz 1rz
1A2 1s0 1r0 1s3 1s2 1A3 1s4 1V2 0x2 2own 1s5 1r3 1r2 1A4 0k9 1r4 1s6 1r6 2e 1r5 0uz 2mm 2y0 2y1 2y2 2y3 2y4 2and0 1s7
1r7 1bs0 2A0 2u0 1sc0 1ki0 1kl0 1ku0 1gl0 1gb0 1lg0 1cl0 1lg1 1cl1 1send 2A1 1ac0 1lg2 2V0 1cl2 2V1 1ac1 1sw 2sz 2s0
2s4 1ac2 1x0 2V2 1x1 2s5 2rz 2A2 2s2 3e 2r4 1uz 3mm 2V3 3y0 3y1 3y2 3y3 3y4 2r5 3and0 3u0 1x2 3own 2A3 2r0 2s6 2A4 2r2
2r6 2s3 2r3 2s7 2r7 2bs0 3A0 3A1 3V0 2sc0 2ki0 2kl0 2ku0 2gl0 2gb0 2lg0 2cl0 2send 2lg1 2cl1 2ac0 2lg2 3V1 2cl2 3V2
2ac1 2sw 2ac2 2x0 3sz 3s0 3s4 3A2 3rz 3A3 3s5 3s2 2x1 2x2 4e 3V3 2uz 3r4 3r5 4mm 4y0 4y1 4y3 4y2 4y4 4and0 4u0 3s6 3A4
3r6 3r0 3r2 3s7 3r7 3s3 3r3 3bs0 4own 4A0 4A1 4A3 4sz 4A2 4rz 4V0 3sc0 3ki0 3kl0 3ku0 3gl0 3gb0 3send 3lg0 3cl0 3lg1
3cl1 3lg2 3cl2 4V1 3ac0 3ac1 3sw 4s0 4s4 4r0 3ac2 3x0 4V2 4s5 5e 5mm 3x1 3x2 4s2 4A4 4r2 4V3 4r4 5y0 5y3 5y1 5y2 3uz
5y4 4r5 5and0 5u0 4s6 4r6 4s3 4s7 4r3 4r7 4bs0 5A0 5own 4pre 5pre 5A1 5V0 5V2 4sc0 5V1 4ki0 4kl0 4ku0 4gl0 4lg1 5s5
5r5 4tt0 5s4 5s0 5sz 4v0 5A2 5rz 5s2 4gb0 4cl1 4lg0 5r4 4a0 4lg2 4cl0 5V3 5r0 4ac1 5up 5A3 5r2 5s3 5r3 5bs0 4a1 4cl2
4a2 4ac0 5sc0 5ki0 5kl0 5ku0 5gl0 5lg0 4ac2 5A4 5s7 5r7 5s6 5r6 5bs1 5um 4v1 5cl0 5ac0 5lg1 5sc1 5gb0 5ki1 5cl1 5kl1
5tt0 5ku1 5tt1 5ac1 5gl1 5gb1 5lg2 5a0 5v0 5v1 5cl2 5x2 5a1 5a2
"""

PLAN = {
    "ch": [[(0, 8)]] * 5 + [[(0, 6), (6, 8)]],
    "lp": [[(0, 48), (48, 96), (96, 128)]] * 6,
    "lo": [C(3)] + [C(4)] * 5,
    "mid": [C(6) + 40, C(6) + 72, C(6) + 32, C(6) + 32, C(6) + 32, C(6) + 16],
    "units": [("z", "a", 0, 128), ("0", "a", C(0), C(2)), ("4", "v", C(4), C(5)), ("5", "v", C(5), C(6)),
              ("2", "a", C(2), C(3)), ("3", "v", C(3), C(4)), ("6", "a", C(6), C(7)), ("7", "v", C(7), C(8))],
    "direct": [(5, 2)],
    "cost": {"cy": 1.04, "ga": 1.56, "pe": 0.525, "add": 1.5},
    "tau": {_s: _i for _i, _s in enumerate(ORDER.split())},
}

SCRATCH = {}
for _x in range(2):
    for _p in range(2):
        SCRATCH["bk%d%d" % (_x, _p)] = ("sbuf", [128, 4096], "bfloat16")
    SCRATCH["G%d" % _x] = ("sbuf", [128, 12288], "bfloat16")
    SCRATCH["U%d" % _x] = ("sbuf", [128, 768], "uint16")
    for _t in range(RO):
        SCRATCH["S%d%d" % (_x, _t)] = ("sbuf", [128, 896], "int32")
        SCRATCH["land%d%d" % (_x, _t)] = ("sbuf", [128, 256], "int32")
    for _n, _w, _d in (("S%d3", 128, "int32"), ("xi%d", 256, "int32"), ("xf%d", 256, "float32"), ("sf%d", 256, "int32"),
                       ("selA%d", 128, "float32"), ("KS%d", 64, "float32"), ("KI%d", 32, "int32"), ("KL%d", 32, "int32"),
                       ("KU%d", 32, "uint16"), ("UL%d", 128, "uint16"), ("DT%d", 2048, "bfloat16"),
                       ("NXF%d", 128, "float32"), ("TT%d", 8, "float32"), ("AI%d", 128, "int32"), ("AJ%d", 128, "int32"),
                       ("AF%d", 128, "float32"), ("VR%d", 128, "float32"), ("TH%d", 128, "int32"), ("TJ%d", 128, "int32"),
                       ("PG%d", 8, "int32"), ("PH%d", 8, "int32"), ("PJ%d", 8, "int32"), ("PU%d", 8, "uint16"),
                       ("PR%d", 128, "int32"), ("cap%d", 128, "bfloat16"), ("E%d", 128, "float32")):
        SCRATCH[_n % _x] = ("sbuf", [128, _w], _d)
    SCRATCH["caprep%d" % _x] = ("sbuf", [128, 8, 80], "bfloat16")
    SCRATCH["R%d" % _x] = ("sbuf", [128, 8, 128], "bfloat16")
    SCRATCH["YI%d" % _x] = ("sbuf", [128, 8, 80], "int32")
for _n, _w, _d in (("AT", 384, "int32"), ("ATf", 384, "float32"), ("D1", 64, "float32"), ("Sel", 15 * 128, "float32"),
                   ("JA", 128, "float32"), ("JB", 144, "float32"), ("JS", 128, "float32"), ("JD", 128, "int32"),
                   ("ID", 128, "bfloat16"), ("NI", 128, "bfloat16"), ("NI32", 128, "float32"), ("BS", 144, "bfloat16"),
                   ("pc", 4, "int32"), ("pd", 4, "int32"), ("col", 8, "float32"), ("W2", 256, "float32")):
    SCRATCH[_n] = ("sbuf", [128, _w], _d)
for _b in range(8):
    SCRATCH["P%d" % _b] = ("psum", [128, 512], "float32")

SEMAPHORES = ["cv", "ca", "cp", "cg", "snd", "ld_a", "ld_th"]
for _x in range(2):
    SEMAPHORES += [_n % _x for _n in ("ld_x%d", "ld_pg%d", "ld_pr%d", "ld_b%d", "pre%d", "oa%d", "ov%d")]
    for _t in range(RO):
        SEMAPHORES += ["arr%d%d" % (_x, _t), "sw%d%d" % (_x, _t), "own%d%d" % (_x, _t)]
        for _c in range(3):
            SEMAPHORES += ["ac%d%d%d" % (_x, _t, _c), "bs%d%d%d" % (_x, _t, _c)]


def rank_program(g, core, T, topo):
    rank = T.rank_of(core)
    if rank is None:
        return
    A = AluOpType
    AF = ActivationFunctionType
    Q = {"g": g, "v": g.vector, "a": g.scalar, "p": g.tensor, "s": g.sync, "x": None}
    CS = {"g": "cg", "v": "cv", "a": "ca", "p": "cp"}
    LP, K = PLAN["lp"], PLAN["cost"]
    OPS = []
    acc = {}
    bank = {}
    group = {}
    now = [""]

    def step(n, name):
        now[0] = "%d%s" % (n, name)

    def reg(r):
        return (r[0], r[1], r[2], r[3] if len(r) > 3 else 0, r[4] if len(r) > 3 else 128)

    def op(q, call, reads=(), writes=(), banks=(), dma=None, inc=16, cost=0.0, after=()):
        me = len(OPS)
        deps, order = set(), set(after)
        for rs, w in ((reads, False), (writes, True)):
            for r in rs:
                n, lo, hi, pl, ph = reg(r)
                for (l2, h2, p2, q2, w2, o) in acc.get(n, ()):
                    if (w or w2) and l2 < hi and lo < h2 and p2 < ph and pl < q2:
                        s = OPS[o]["dma"]
                        if s is None or s == "snd":
                            deps.add(o)
                        elif s != dma:
                            deps.update(group[s])
        for b in banks:
            for qq, o in bank.get(b, {}).items():
                (deps if qq != q else order).add(o)
            bank.setdefault(b, {})[q] = me
        for rs, w in ((reads, False), (writes, True)):
            for r in rs:
                n, lo, hi, pl, ph = reg(r)
                lst = acc.setdefault(n, [])
                if w:
                    lst[:] = [e for e in lst if not (lo <= e[0] and e[1] <= hi and pl <= e[2] and e[3] <= ph)]
                lst.append((lo, hi, pl, ph, w, me))
        if dma is not None:
            group.setdefault(dma, []).append(me)
        OPS.append({"q": q, "calls": call if isinstance(call, list) else [call], "deps": deps, "order": order,
                    "dma": dma, "inc": inc, "cost": cost, "step": now[0]})
        return me

    def in_order(tau):
        place = [tau.get(o["step"], -1.0) for o in OPS]
        for i in range(len(OPS) - 1, -1, -1):
            for j in OPS[i]["deps"] | OPS[i]["order"]:
                place[j] = min(place[j], place[i])
        return sorted(range(len(OPS)), key=lambda i: (place[i], i))

    def emit(seq):
        total = {}
        clock = {q: {} for q in Q}
        tok, snap = {}, {}

        def wait(q, sem, val):
            if clock[q].get(sem, 0) >= val:
                return
            Q[q].wait_ge(T.sem[sem], val)
            for k, v in snap.get((sem, val), {}).items():
                if clock[q].get(k, 0) < v:
                    clock[q][k] = v
            clock[q][sem] = val
        for i in seq:
            o = OPS[i]
            q = o["q"]
            best = {}
            for j in o["deps"]:
                sem, val = tok[j]
                best[sem] = max(best.get(sem, 0), val)
            for sem, val in sorted(best.items(), key=lambda e: (e[0] not in CS.values(), e[0])):
                wait(q, sem, val)
            if o["dma"] is None:
                sem = CS[q]
                for c in o["calls"]:
                    c().then_inc(T.sem[sem], 1)
                    total[sem] = total.get(sem, 0) + 1
                snap[(sem, total[sem])] = dict(clock[q])
            else:
                sem = o["dma"]
                ins = o["calls"][0]() if q != "x" else None
                if ins is not None:
                    ins.then_inc(T.sem[sem], o["inc"])
                s = dict(snap.get((sem, total.get(sem, 0)), {}))
                total[sem] = total.get(sem, 0) + o["inc"]
                for k, v in clock[q].items():
                    s[k] = max(s.get(k, 0), v)
                snap[(sem, total[sem])] = s
            tok[i] = (sem, total[sem])
        for sem in total:
            wait("g", sem, total[sem])

    V = g.vector
    RCOL, NEGR, C15, HSH, H128, M1 = 0, 1, 2, 3, 4, 5

    def cc(j):
        return T.col[:, j:j + 1]

    def cr(j):
        return ("col", j, j + 1)

    def width(writes):
        return sum(w[2] - w[1] for w in writes)

    def vcost(writes, rate):
        return (60 + width(writes) * K["ga"] if rate == "g" else max(64, width(writes) * rate)) * K["cy"]

    def ts(out, in0, s1, s2, o0, o1, reads, writes, banks=(), rate=1):
        if o1 is None:
            op("v", lambda: V.tensor_scalar(out, in0, s1, None, o0), reads, writes, banks, cost=vcost(writes, rate))
        else:
            op("v", lambda: V.tensor_scalar(out, in0, s1, s2, o0, o1), reads, writes, banks, cost=vcost(writes, rate))

    def tt(out, in0, in1, o, reads, writes, banks=(), rate=None):
        op("v", lambda: V.tensor_tensor(out, in0, in1, o), reads, writes, banks,
           cost=vcost(writes, rate or (1 if banks else 2)))

    def cp(out, in_, reads, writes, banks=(), rate=1):
        op("v", lambda: V.tensor_copy(out, in_), reads, writes, banks, cost=vcost(writes, rate))

    def ms(ap, val, writes):
        op("v", lambda: V.memset(ap, val), (), writes, cost=vcost(writes, 1))

    def act(out, in_, func, reads, writes, banks=(), rate=1, **kw):
        op("a", lambda: g.scalar.activation(out, in_, func, **kw), reads, writes, banks, cost=vcost(writes, rate))

    def mms(items, reads, b):
        calls = [lambda e=e, j=j: g.tensor.matmul(e[0], e[1], e[2], j == 0, j == len(items) - 1)
                 for j, e in enumerate(items)]
        op("p", calls, reads, (), (b,), cost=sum(e[3] for e in items) * K["pe"])

    def dma(q, out, in_, sem, reads, writes, size, add=False):
        by = sum((w[2] - w[1]) * (w[4] - w[3] if len(w) > 3 else 128) for w in writes) * size
        if add:
            op(q, lambda: Q[q].dma_start(out, in_, accum_op=A.add, max_dma_last_dim=4096), reads, writes, dma=sem,
               cost=by * K["add"])
        else:
            op(q, lambda: Q[q].dma_start(out, in_), reads, writes, dma=sem, cost=by)

    def iota(out, pattern, base, chan, writes, flt=True):
        cost = 130 + 2 * width(writes) * K["cy"]
        if flt:
            op("g", lambda: g.iota(out, pattern, base, chan, allow_small_or_imprecise_dtypes=True), (), writes, cost=cost)
        else:
            op("g", lambda: g.iota(out, pattern, base, chan), (), writes, cost=cost)

    def P(b):
        return T["P%d" % b]

    def equal(name, lo, hi, src, s0, s1, val, times=None):
        ts(T[name][:, lo:hi], T[src][:, s0:s1], cc(val[0]) if isinstance(val, tuple) else float(val), times, A.is_equal,
           None if times is None else A.mult, [(src, s0, s1)] + ([cr(val[0])] if isinstance(val, tuple) else []),
           [(name, lo, hi)])

    def load_turned(q, n, src, X, w, sem, size, gate=()):
        r0 = 64 * X
        dma(q, T[n][0:64, :], src[r0:r0 + 64, :], sem, gate, [(n, 0, 2 * w, 0, 64)], size)
        dma(q, T[n][64:128, 0:w], src[r0:r0 + 64, w:2 * w], sem, gate, [(n, 0, w, 64, 128)], size)
        dma(q, T[n][64:128, w:2 * w], src[r0:r0 + 64, 0:w], sem, gate, [(n, w, 2 * w, 64, 128)], size)

    def load_halves(q, n, src, X, w, sem):
        for h in range(2):
            dma(q, T[n][64 * h:64 * h + 64, :], src[64 * X:64 * X + 64, w * h:w * h + w], sem, (),
                [(n, 0, w, 64 * h, 64 * h + 64)], 4)

    def exchange(X, t):
        dst = T.cores[(rank - 1 - t % (N - 1)) % N]
        frm = T.cores[(rank + 1 + t % (N - 1)) % N]
        rid, pid, _se = topo.addr(dst)
        eng = topo.engines(core, dst)[::2]
        mask = sum(1 << e for e in eng)
        n = "land%d%d" % (X, t)
        w = 256 if t == 0 else 128
        sn = "sf%d" % X if t == 0 else "S%d%d" % (X, t)

        def call():
            g.remote_dma(T[n][:, 0:w], T[sn][:, 0:w], T.sem["arr%d%d" % (X, t)], T.sem.snd, pid, rid, mask)
            return None
        sent = op("g", call, [(sn, 0, w)], (), dma="snd", inc=len(eng), cost=512.0 * w)
        op("x", None, (), [(n, 0, w)], dma="arr%d%d" % (X, t), inc=len(topo.engines(frm, core)[::2]), after=(sent,))
        if t > 0:
            step(2 * t + X - 2, "sw")
            for h in range(2):
                o = 64 - 64 * h
                dma("s", T[n][o:o + 64, 128:256], T[n][64 * h:64 * h + 64, 0:128], "sw%d%d" % (X, t),
                    [(n, 0, 128, 64 * h, 64 * h + 64)], [(n, 128, 256, o, o + 64)], 4)

    def first_send(X):
        xf, sf, sa, b = "xf%d" % X, "sf%d" % X, "selA%d" % X, 6 + X
        mms([(P(b)[:, 0:256], T[sa][0:16, :], T.ATf[0:16, 0:256], 1024)], [(sa, 0, 128), ("ATf", 0, 256)], b)
        ts(T[xf][:, :], T["xi%d" % X][:, :], cc(HSH), None, A.add, None, [("xi%d" % X, 0, 256), cr(HSH)], [(xf, 0, 256)])
        tt(T[sf][:, :], T[xf][:, :], P(b)[:, 0:256], A.subtract, [(xf, 0, 256)], [(sf, 0, 256)], (b,))
        exchange(X, 0)

    def first_lists(X):
        sf, s, u = "sf%d" % X, "S%d0" % X, "U%d" % X
        pg, ph, pj, pu = "PG%d" % X, "PH%d" % X, "PJ%d" % X, "PU%d" % X
        ts(T[s][:, 0:128], T[sf][:, 0:128], 4095, None, A.bitwise_and, None, [(sf, 0, 128)], [(s, 0, 128)])
        ts(T[ph][:, :], T[pg][:, :], cc(H128), None, A.add, None, [(pg, 0, 8), cr(H128)], [(ph, 0, 8)])
        cp(T[u][:, 0:128], T[s][:, 0:128], [(s, 0, 128)], [(u, 0, 128)])
        ts(T[pj][:, :], T[ph][:, :], 255, None, A.bitwise_and, None, [(ph, 0, 8)], [(pj, 0, 8)])
        cp(T["cap%d" % X][:, :], T["PR%d" % X][:, :], [("PR%d" % X, 0, 128)], [("cap%d" % X, 0, 128)])
        cp(T[pu][:, :], T[pj][:, :], [(pj, 0, 8)], [(pu, 0, 8)])

    def caps(X):
        r, sa, cap, th, tj, b = "R%d" % X, "selA%d" % X, "cap%d" % X, "TH%d" % X, "TJ%d" % X, 6 + X
        mms([(P(b)[:, 0:128], T[sa][0:16, :], T.ATf[0:16, 256:384], 512)], [(sa, 0, 128), ("ATf", 256, 384)], b)
        for k in range(5):
            cp(T["caprep%d" % X][:, :, 16 * k:16 * k + 16], T[cap][:, :], [(cap, 0, 128)],
               [("caprep%d" % X, 80 * c + 16 * k, 80 * c + 16 * k + 16) for c in range(8)], rate=0.5)
        ts(T[th][:, :], P(b)[:, 0:128], cc(C15), None, A.add, None, [cr(C15)], [(th, 0, 128)], (b,))
        ms(T[r][:, :, 96:112], 256.0, [(r, 128 * c + 96, 128 * c + 112) for c in range(8)])
        ts(T[tj][:, :], T[th][:, :], 4, None, A.arith_shift_right, None, [(th, 0, 128)], [(tj, 0, 128)])
        ident(X, 0)
        tt(T[r][:, :, 112:128], T[cap][:, :], T[tj][:, :], A.subtract, [(cap, 0, 128), (tj, 0, 128)],
           [(r, 128 * c + 112, 128 * c + 128) for c in range(8)])

    def ident(X, t):
        ts(T["S%d%d" % (X, t)][:, 768:896], T.JD[:, :], cc(RCOL), None, A.add, None, [("JD", 0, 128), cr(RCOL)],
           [("S%d%d" % (X, t), 768, 896)])

    def turn(X):
        pu, xf = "PU%d" % X, "xf%d" % X
        tt(T["NXF%d" % X][:, :], T.W2[:, 0:256].indirect(T[pu][:, 0:8]), T[xf][:, 0:128], A.subtract,
           [("W2", 0, 256), (pu, 0, 8), (xf, 0, 128)], [("NXF%d" % X, 0, 128)], rate="g")

    def prep(n):
        X, t = n % 2, n // 2
        ld, xf, s, u, e, y = "land%d%d" % (X, t), "xf%d" % X, "S%d%d" % (X, t), "U%d" % X, "E%d" % X, "YI%d" % X
        pu = "PU%d" % X
        sub = xf if t == 0 else "NXF%d" % X
        step(n, "e")
        tt(T[e][:, :], T[ld][:, 0:256].indirect(T[pu][:, 0:8]), T[sub][:, 0:128], A.subtract if t == 0 else A.add,
           [(ld, 0, 256), (pu, 0, 8), (sub, 0, 128)], [(e, 0, 128)], rate="g")
        step(n, "mm")
        for k in range(5):
            i = 5 * t + k
            mms([(P(6 + k // 3)[:, 128 * (k % 3):128 * (k % 3) + 128], T.Sel[:, 128 * i:128 * i + 128], T[e][:, :], 512)],
                [("Sel", 128 * i, 128 * i + 128), (e, 0, 128)], 6 + k // 3)
        for k in range(5):
            step(n, "y%d" % k)
            tt(T[y][:, :, 16 * k:16 * k + 16], P(6 + k // 3)[:, 128 * (k % 3):128 * (k % 3) + 128], T[xf][:, 0:128],
               A.add, [(xf, 0, 128)], [(y, 80 * c + 16 * k, 80 * c + 16 * k + 16) for c in range(8)], (6 + k // 3,))
        for j, (c0, c1) in enumerate(((0, 2), (2, 8)) if n == 0 else ((0, 8),)):
            step(n, "and%d" % j)
            ts(T[s][:, C(c0):C(c1)], T[y][:, c0:c1, :], 4095, None, A.bitwise_and, None, [(y, 80 * c0, 80 * c1)],
               [(s, C(c0), C(c1))])
            step(n, "u%d" % j)
            cp(T[u][:, C(c0):C(c1)], T[s][:, C(c0):C(c1)], [(s, C(c0), C(c1))], [(u, C(c0), C(c1))])

    def gat(n, e, a, b):
        X, t = n % 2, n // 2
        bk = "bk%d%d" % (X, t % 2)
        out = T["G%d" % X][:, 16 * a:16 * b]
        win = T[bk][:, 0:4096].indirect(T["U%d" % X][:, a:b])
        rd, wr = [(bk, 0, 4096), ("U%d" % X, a, b)], [("G%d" % X, 16 * a, 16 * b)]
        if e == "v":
            cp(out, win, rd, wr, rate="g")
        else:
            act(out, win, AF.Copy, rd, wr, rate="g")

    def sums(n, name, e, bnk, a, b):
        X = n % 2
        r, cn = "R%d" % X, "caprep%d" % X
        if b <= 128:
            out, wr = T[r][:, a // 16:b // 16, 0:16], [(r, 128 * c, 128 * c + 16) for c in range(a // 16, b // 16)]
            cap, crd = T["cap%d" % X][:, a:b], ("cap%d" % X, a, b)
        else:
            c0, c1 = (a - 128) // 80, (b - 128) // 80
            out, wr = T[r][:, c0:c1, 16:96], [(r, 128 * c + 16, 128 * c + 96) for c in range(c0, c1)]
            cap, crd = T[cn][:, c0:c1, :], (cn, a - 128, b - 128)
        ps = P(bnk)[:, 0:b - a]
        step(n, "s" + name)
        mms([(ps, T.ID[:, :], cap, b - a)] +
            [(ps, T.NI[:, :], T["G%d" % X][:, 16 * a + i:16 * b:16], b - a) for i in range(16)],
            [("ID", 0, 128), ("NI", 0, 128), crd, ("G%d" % X, 16 * a, 16 * b)], bnk)
        step(n, "r" + name)
        if e == "v":
            ts(out, ps, 0.0, None, A.max, None, (), wr, (bnk,))
        else:
            act(out, ps, AF.Relu, (), wr, (bnk,))

    def select(n, ch):
        X, t = n % 2, n // 2
        c0, c1 = PLAN["ch"][n][ch]
        nc = c1 - c0
        k0 = 16 * ch
        ks, ki, kl, ku, s = "KS%d" % X, "KI%d" % X, "KL%d" % X, "KU%d" % X, "S%d%d" % (X, t)
        sn, ul = "S%d%d" % (X, t + 1), "UL%d" % X
        d0, d1 = 16 * c0, 16 * c1
        step(n, "bs%d" % ch)
        mms([(P(4 + ch)[:, 0:8 * nc], T.BS[:, 15 - r:143 - r], T["R%d" % X][:, c0:c1, r:128:16], 64) for r in range(16)],
            [("BS", 0, 144), ("R%d" % X, 128 * c0, 128 * c1)], 4 + ch)
        step(n, "sc%d" % ch)
        op("v", lambda: V.tensor_tensor_scan(T[ks][:, 8 * c0:8 * c1], P(4 + ch)[:, 0:8 * nc], T.D1[:, 8 * c0:8 * c1],
                                             float(2 * BIG), A.min, A.add),
           [("D1", 0, 64)], [(ks, 8 * c0, 8 * c1)], (4 + ch,), cost=64 * K["cy"])
        step(n, "ki%d" % ch)
        cp(T[ki][:, k0 + nc:k0 + 2 * nc], T[ks][:, 8 * c0 + 7:8 * c1:8], [(ks, 8 * c0, 8 * c1)],
           [(ki, k0 + nc, k0 + 2 * nc)])
        cp(T[ki][:, k0:k0 + nc], T[ks][:, 8 * c0 + 5:8 * c1:8], [(ks, 8 * c0, 8 * c1)], [(ki, k0, k0 + nc)])
        step(n, "kl%d" % ch)
        ts(T[kl][:, k0:k0 + 2 * nc], T[ki][:, k0:k0 + 2 * nc], 1023, None, A.bitwise_and, None,
           [(ki, k0, k0 + 2 * nc)], [(kl, k0, k0 + 2 * nc)])
        step(n, "ku%d" % ch)
        ts(T[ku][:, k0:k0 + 2 * nc], T[kl][:, k0:k0 + 2 * nc], cc(RCOL), None, A.add, None,
           [(kl, k0, k0 + 2 * nc), cr(RCOL)], [(ku, k0, k0 + 2 * nc)])
        step(n, "gl%d" % ch)
        cp(T[ul][:, d0:d1], T[s][:, 0:896].indirect(T[ku][:, k0 + nc:k0 + 2 * nc]),
           [(s, 0, 896), (ku, k0 + nc, k0 + 2 * nc)], [(ul, d0, d1)], rate="g")
        step(n, "gb%d" % ch)
        cp(T[sn][:, d0:d1], T[s][:, 0:896].indirect(T[ku][:, k0:k0 + nc]),
           [(s, 0, 896), (ku, k0, k0 + nc)], [(sn, d0, d1)], rate="g")
        if t == RO - 1:
            step(n, "tt%d" % ch)
            tt(T["TT%d" % X][:, c0:c1], T[ki][:, k0:k0 + nc], T[kl][:, k0:k0 + nc], A.subtract,
               [(ki, k0, k0 + nc), (kl, k0, k0 + nc)], [("TT%d" % X, c0, c1)])

    def own(n):
        X, t = n % 2, n // 2
        ob, nb = "bk%d%d" % (X, t % 2), "bk%d%d" % (X, (t + 1) % 2)
        step(n, "own")
        dma("s", T[nb][:, 0:2048], T[ob][:, 0:2048], "own%d%d" % (X, t), [(ob, 0, 2048)], [(nb, 0, 2048)], 2)
        if t == RO - 1:
            step(n, "pre")
            w = 16 * min([LP[n][j][0] for j in range(len(LP[n])) if (n, j) in PLAN["direct"]] + [128])
            for h in range(2):
                dma("s", T.yb[64 * X:64 * X + 64, 2048 * h:2048 * h + w], T[ob][64 * h:64 * h + 64, 0:w],
                    "pre%d" % X, [(ob, 0, w, 64 * h, 64 * h + 64)],
                    [("yb", 2048 * h, 2048 * h + w, 64 * X, 64 * X + 64)], 2)

    def learn(n, j):
        X, t = n % 2, n // 2
        bk, nb, d, ul = "bk%d%d" % (X, t % 2), "bk%d%d" % (X, (t + 1) % 2), "DT%d" % X, "UL%d" % X
        a, b = 16 * LP[n][j][0], 16 * LP[n][j][1]
        ac = "ac%d%d%d" % (X, t, j)
        win = T[bk][:, 0:4096].indirect(T[ul][:, a // 16:b // 16])
        rd = [(bk, 0, 4096), (ul, a // 16, b // 16)]
        if (n, j) in PLAN["direct"]:
            ob = "bk%d%d" % (1 - X, (t + 1) % 2)
            step(n, "um")
            act(T[ob][:, a:b], T[nb][:, a:b], AF.Identity, [(nb, a, b), cr(M1)], [(ob, a, b)], bias=cc(M1))
            step(n, "up")
            act(P(7)[:, 0:b - a], T[nb][:, a:b], AF.Identity, [(nb, a, b), cr(M1 + 1)], [("P7", a, b)], (7,),
                bias=cc(M1 + 1))
            step(n, "lg%d" % j)
            tt(T[d][:, a:b], win, T[ob][:, a:b], A.max, rd + [(ob, a, b)], [(d, a, b)], rate="g")
            step(n, "cl%d" % j)
            tt(T[d][:, a:b], T[d][:, a:b], P(7)[:, 0:b - a], A.min, [(d, a, b)], [(d, a, b)], (7,))
            step(n, "x%d" % j)
            for h in range(2):
                dma("sa"[h], T.yb[64 * X:64 * X + 64, 2048 * h + a:2048 * h + b], T[d][64 * h:64 * h + 64, a:b], ac,
                    [(d, a, b, 64 * h, 64 * h + 64)], [("yb", 2048 * h + a, 2048 * h + b, 64 * X, 64 * X + 64)], 2)
            return
        step(n, "lg%d" % j)
        tt(T[d][:, a:b], win, T[nb][:, a:b], A.subtract, rd + [(nb, a, b)], [(d, a, b)], rate="g")
        step(n, "cl%d" % j)
        ts(T[d][:, a:b], T[d][:, a:b], -1.0, 1.0, A.max, A.min, [(d, a, b)], [(d, a, b)], rate=0.5)
        step(n, "ac%d" % j)
        if t < RO - 1:
            dma("g", T[nb][:, a:b], T[d][:, a:b], ac, [(d, a, b)], [(nb, a, b)], 2, True)
            step(n, "x%d" % j)
            for h in range(2):
                o = 64 - 64 * h
                dma("s", T[nb][o:o + 64, 2048 + a:2048 + b], T[nb][64 * h:64 * h + 64, a:b], "bs%d%d%d" % (X, t, j),
                    [(nb, a, b, 64 * h, 64 * h + 64)], [(nb, 2048 + a, 2048 + b, o, o + 64)], 2)
        else:
            for h in range(2):
                dma("g", T.yb[64 * X:64 * X + 64, 2048 * h + a:2048 * h + b], T[d][64 * h:64 * h + 64, a:b], ac,
                    [(d, a, b, 64 * h, 64 * h + 64)], [("yb", 2048 * h + a, 2048 * h + b, 64 * X, 64 * X + 64)], 2, True)

    def finish(n):
        X = n % 2
        s, ai, aj, af, vr = "S%d3" % X, "AI%d" % X, "AJ%d" % X, "AF%d" % X, "VR%d" % X
        step(n, "a0")
        tt(T[ai][:, :], T["xf%d" % X][:, 0:128], T[s][:, :], A.subtract, [("xf%d" % X, 0, 128), (s, 0, 128)],
           [(ai, 0, 128)])
        step(n, "a1")
        ts(T[aj][:, :], T[ai][:, :], 4095, None, A.bitwise_and, None, [(ai, 0, 128)], [(aj, 0, 128)])
        step(n, "a2")
        cp(T[af][:, :], T[aj][:, :], [(aj, 0, 128)], [(af, 0, 128)])
        for h in range(2):
            dma("s", T.ya[4 * X:4 * X + 4, 128 * h:128 * h + 128], T[af][64 * h:64 * h + 64:16, :], "oa%d" % X,
                [(af, 0, 128)], [("ya", 128 * h, 128 * h + 128, 4 * X, 4 * X + 4)], 4)
        step(n, "v0")
        mms([(P(6)[0:8, 0:128], T.BS[:, 15:143:16], T["cap%d" % X][:, :], 128)] +
            [(P(6)[0:8, r:128:16], T.NI32[:, r:128:16], T["TT%d" % X][:, :], 32) for r in range(16)],
            [("BS", 0, 144), ("cap%d" % X, 0, 128), ("NI32", 0, 128), ("TT%d" % X, 0, 8)], 6)
        step(n, "v1")
        act(T[vr][0:8, :], P(6)[0:8, 0:128], AF.Copy, (), [(vr, 0, 128)], (6,), scale=1.0 / 1024)
        for h in range(2):
            dma("s", T.yv[4 * X:4 * X + 4, 128 * h:128 * h + 128], T[vr][4 * h:4 * h + 4, :], "ov%d" % X,
                [(vr, 0, 128)], [("yv", 128 * h, 128 * h + 128, 4 * X, 4 * X + 4)], 4)

    dma("a", T.AT[0:8, 0:256], T.a0[:, :], "ld_a", (), [("AT", 0, 256, 0, 8)], 4)
    dma("a", T.AT[8:16, 0:128], T.a0[:, 128:256], "ld_a", (), [("AT", 0, 128, 8, 16)], 4)
    dma("a", T.AT[8:16, 128:256], T.a0[:, 0:128], "ld_a", (), [("AT", 128, 256, 8, 16)], 4)
    load_turned("s", "xi0", T.ct, 0, 128, "ld_x0", 4)
    load_halves("a", "PG0", T.pg, 0, 8, "ld_pg0")
    load_halves("a", "PR0", T.pr, 0, 128, "ld_pr0")
    load_turned("s", "bk00", T.bk, 0, 2048, "ld_b0", 2)
    dma("a", T.AT[0:8, 256:384], T.th[:, 0:128], "ld_th", (), [("AT", 256, 384, 0, 8)], 4)
    dma("a", T.AT[8:16, 256:384], T.th[:, 128:256], "ld_th", (), [("AT", 256, 384, 8, 16)], 4)
    load_turned("s", "xi1", T.ct, 1, 128, "ld_x1", 4)
    load_halves("a", "PG1", T.pg, 1, 8, "ld_pg1")
    load_halves("a", "PR1", T.pr, 1, 128, "ld_pr1")
    load_turned("s", "bk10", T.bk, 1, 2048, "ld_b1", 2, [("bk00", 0, 1)])

    iota(T.JA[:, :], [[-8, 2], [-1, 4], [0, 16]], 0, 1, [("JA", 0, 128)])
    iota(T.JS[:, :], [[-16, 8], [0, 16]], 0, 1, [("JS", 0, 128)])
    iota(T.pc[:, 0:1], [[0, 1]], 0, 1, [("pc", 0, 1)], False)
    iota(T.JB[:, :], [[1, 144]], -15, -1, [("JB", 0, 144)])
    iota(T.JD[:, :], [[16, 128]], 0, 0, [("JD", 0, 128)], False)
    for h in range(2):
        ms(T.col[64 * h:64 * h + 64, HSH:HSH + 1], 8192.0 + 2048 * h, [("col", HSH, HSH + 1, 64 * h, 64 * h + 64)])
        ms(T.col[64 * h:64 * h + 64, H128:H128 + 1], 128.0 * h, [("col", H128, H128 + 1, 64 * h, 64 * h + 64)])
    ms(T.D1[:, :], -16.0, [("D1", 0, 64)])
    ms(cc(M1), -1.0, [cr(M1)])
    ms(cc(M1 + 1), 1.0, [cr(M1 + 1)])
    for h in range(2):
        ms(T.W2[:, 128 * h:128 * h + 128], 4096.0 + 2048 * h, [("W2", 128 * h, 128 * h + 128)])
        equal("selA%d" % h, 0, 128, "JA", 0, 128, 4 * h)
    for i in range(5):
        equal("Sel", 128 * i, 128 * i + 128, "JS", 0, 128, i)
    ts(T.pd[:, 0:1], T.pc[:, 0:1], 15, None, A.bitwise_and, None, [("pc", 0, 1)], [("pd", 0, 1)])
    equal("ID", 0, 128, "JB", 15, 143, 0)
    cp(cc(RCOL), T.pd[:, 0:1], [("pd", 0, 1)], [cr(RCOL)])
    ts(cc(NEGR), T.pd[:, 0:1], -1.0, None, A.mult, None, [("pd", 0, 1)], [cr(NEGR)])
    ts(cc(C15), T.pd[:, 0:1], -1.0, 15.0, A.mult, A.add, [("pd", 0, 1)], [cr(C15)])
    equal("NI", 0, 128, "JB", 15, 143, 0, -1.0)
    cp(T.ATf[0:16, 0:256], T.AT[0:16, 0:256], [("AT", 0, 256, 0, 16)], [("ATf", 0, 256)])
    first_send(0)
    iota(T.D1[:, 0:64:8], [[-64, 8]], -128, 0, [("D1", 0, 8)])
    iota(T.D1[:, 5:64:8], [[80, 8]], 192, 0, [("D1", 8, 16)])
    iota(T.D1[:, 6:64:8], [[-16, 8]], -768, 0, [("D1", 16, 24)])
    iota(T.D1[:, 7:64:8], [[16, 8]], BIG + 768, 0, [("D1", 24, 32)])
    first_lists(0)
    equal("BS", 0, 144, "JB", 0, 144, (NEGR,), 1024.0)
    for i in range(5, 10):
        equal("Sel", 128 * i, 128 * i + 128, "JS", 0, 128, i)
    equal("NI32", 0, 128, "JB", 15, 143, 0, -1.0)
    cp(T.ATf[0:16, 256:384], T.AT[0:16, 256:384], [("AT", 256, 384, 0, 16)], [("ATf", 256, 384)])
    caps(0)
    turn(0)
    first_send(1)
    first_lists(1)
    caps(1)
    turn(1)
    for j, f in enumerate([lambda: ident(0, 1), lambda: ident(1, 1), lambda: ident(0, 2), lambda: ident(1, 2)] +
                          [lambda i=i: equal("Sel", 128 * i, 128 * i + 128, "JS", 0, 128, i) for i in range(10, 15)]):
        step(0, "k%d" % (j + 1))
        f()

    for n in range(2 * RO):
        X, t = n % 2, n // 2
        lo, mid = PLAN["lo"][n], PLAN["mid"][n]
        prep(n)
        own(n)
        for e, parts in (("a", [(0, 128), (C(0), C(2)), (C(2), lo), (C(6), mid), (C(7), C(8))]),
                         ("v", [(lo, lo + 40), (lo + 40, C(5)), (C(5), C(6)), (mid, C(7))])):
            for j, (a, b) in enumerate(parts):
                step(n, "%s%d" % (e.upper(), j))
                gat(n, e, a, b)
        for j, (name, e, a, b) in enumerate(PLAN["units"]):
            sums(n, name, e, j % 4, a, b)
        for ch in range(len(PLAN["ch"][n])):
            select(n, ch)
        if t < RO - 1:
            step(n, "uz")
            cp(T["U%d" % X][:, 0:128], T["S%d%d" % (X, t + 1)][:, 0:128], [("S%d%d" % (X, t + 1), 0, 128)],
               [("U%d" % X, 0, 128)])
            step(n, "send")
            exchange(X, t + 1)
        for j in range(len(LP[n])):
            learn(n, j)
    finish(2 * RO - 2)
    finish(2 * RO - 1)
    PLAN["out"] = (OPS, in_order)
    if "dry" not in PLAN:
        emit(in_order(PLAN["tau"]))
